import numpy as np
import ml_dtypes


def mxq(x, axis, fmt="e4m3"):
    dtype, down = {"e4m3": (ml_dtypes.float8_e4m3fn, 7), "e5m2": (ml_dtypes.float8_e5m2, 14)}[fmt]
    v = np.moveaxis(np.asarray(x, np.float32).astype(ml_dtypes.bfloat16).astype(np.float64), axis, -1)
    blocks = v.reshape(v.shape[:-1] + (-1, 32))
    amax = np.abs(blocks).max(-1, keepdims=True)
    byte = np.maximum(np.where(amax > 0, np.frexp(amax)[1] - 1 + 127, 0) - down, 1)
    scale = np.exp2(byte - 127.0)
    codes = (blocks / scale).astype(np.float32).astype(dtype).astype(np.float64)
    return np.moveaxis((codes * scale).reshape(v.shape), -1, axis)


WIDE = False


def mx_kscale(k):
    if not WIDE:
        return np.ones(k)
    levels = np.array([10, -10, 5, -5, 0])
    if k % 512:
        return np.exp2(np.random.permutation(np.resize(levels, k // 32))).repeat(32)
    a = np.empty((k // 512, 16))
    for p in range(k // 512):
        a[p, :8] = np.random.permutation(np.resize(levels, 8))
        for g in range(8):
            far = levels[np.abs(levels - a[p, g]) >= 10]
            a[p, g + 8] = far[np.random.randint(len(far))]
    return np.exp2(a.ravel()).repeat(32)


def f64(x):
    return np.asarray(x).astype(np.float64)


def striped(idx):
    return np.tile(idx.reshape(-1, 16).T, (8, 1)).astype(np.uint16)


def unstriped(offs):
    return offs[:16].T.reshape(-1).astype(np.int64)


E2M1 = np.array([0.0, 0.5, 1.0, 1.5, 2.0, 3.0, 4.0, 6.0, -0.0, -0.5, -1.0, -1.5, -2.0, -3.0, -4.0, -6.0])


def pack_weight(w, fmt):
    k, n = w.shape
    w = f64(np.asarray(w, np.float32).astype(ml_dtypes.bfloat16)).reshape(k // 32, 32, n)
    amax = np.abs(w).max(1)
    if fmt == "e4m3":
        byte = np.frexp(amax)[1] - 1 + 127 - 7
    else:
        mant, ex = np.frexp(amax / 6.0)
        byte = np.where(mant > 0.5, ex, ex - 1) + 127
    byte = np.clip(np.where(amax > 0, byte, 1), 1, 254)
    scaled = (w * np.exp2(127.0 - byte)[:, None, :]).reshape(k, n).astype(np.float32)
    by_word = np.ascontiguousarray(scaled.reshape(k // 512, 128, 4, n).transpose(0, 1, 3, 2))
    if fmt == "e4m3":
        words = by_word.astype(ml_dtypes.float8_e4m3fn).view(np.uint8)
    else:
        c = by_word.astype(ml_dtypes.float4_e2m1fn).view(np.uint8) & 0xF
        words = (c[..., 0::2] | (c[..., 1::2] << 4)).reshape(k // 512, 128, 2 * n)
    return np.ascontiguousarray(words), np.ascontiguousarray(byte.astype(np.uint8).reshape(k // 512, 16, n))


def unpack_weight(words, scales, fmt):
    g, _, n = scales.shape
    words = np.ascontiguousarray(words).reshape(g, 128, n, -1)
    if fmt == "e4m3":
        vals = words.view(ml_dtypes.float8_e4m3fn).astype(np.float64)
    else:
        nib = np.empty((g, 128, n, 4), np.uint8)
        nib[..., 0::2] = words & 0xF
        nib[..., 1::2] = words >> 4
        vals = E2M1[nib]
    vals = vals * np.repeat(np.exp2(scales.astype(np.float64) - 127.0), 8, axis=1)[..., None]
    return vals.transpose(0, 1, 3, 2).reshape(g * 512, n)


G, K, M, T, S = 2, 1024, 512, 1024, 256


def setup_inputs():
    n = np.random.standard_normal
    s = mx_kscale(K)[:, None]
    p_w4 = pack_weight(n((K, M)) / np.sqrt(K) / s, "e2m1")
    p_w8 = pack_weight(n((K, M)) / np.sqrt(K) / s, "e4m3")
    return {
        "xT": (n((K, T)) * s).astype(np.float32),
        "c": (n((K, S)) * s).astype(np.float32),
        "w4_words": p_w4[0],
        "w4_scales": p_w4[1],
        "w8_words": p_w8[0],
        "w8_scales": p_w8[1],
        "offs": striped(np.concatenate([np.random.permutation(T)[:S] for _ in range(G)])),
    }


def reference(xT, c, w4_words, w4_scales, w8_words, w8_scales, offs):
    idx = unstriped(offs).reshape(G, S)
    d_ = [mxq(f64(xT)[:, idx[g]] - f64(c), 0, "e4m3") for g in range(G)]
    c_ = mxq(f64(c), 0, "e4m3")
    w4_ = unpack_weight(w4_words, w4_scales, "e2m1")
    w8_ = unpack_weight(w8_words, w8_scales, "e4m3")
    y = np.max([(d.T @ w4_) for d in d_], axis=0) + (c_.T @ w8_)
    return y

@@ -1,0 +1,122 @@
+from contextlib import ExitStack
+
+import concourse.mybir as mybir
+
+G, K, M, T, S = 2, 1024, 512, 1024, 256
+FLOPS = 2 * K * M * S * (G + 1)
+
+F32 = mybir.dt.float32
+BF16 = mybir.dt.bfloat16
+I32 = mybir.dt.int32
+U32 = mybir.dt.uint32
+U16 = mybir.dt.uint16
+U8 = mybir.dt.uint8
+FP8X4 = mybir.dt.float8_e4m3fn_x4
+FP4X4 = mybir.dt.float4_e2m1fn_x4
+ALU = mybir.AluOpType
+
+P = 128
+PACK = 4
+K_PASS = P * PACK
+PASSES = K // K_PASS
+J_TILE = 128
+J_TILES = S // J_TILE
+STRIPE = 16
+
+
+def interleave(engine_copy, grouped, planes):
+    engine_copy(
+        grouped.rearrange("p (c i) t -> p c t i", i=4),
+        planes.rearrange("p t (c i) -> p c t i", i=4),
+    )
+
+
+def tile_list_edge_tm_none_kernel(tc, xT, c, w4_words, w4_scales, w8_words, w8_scales, offs, out):
+    nc = tc.nc
+    with ExitStack() as ctx:
+        keep = ctx.enter_context(tc.tile_pool(name="keep", bufs=1))
+        psum = ctx.enter_context(tc.psum_pool(name="psum", bufs=1))
+
+        offsets = keep.tile([P, G * S // STRIPE], U16, name="offsets")
+        nc.sync.dma_start(offsets[:], offs)
+
+        s4 = keep.tile([P, PASSES, M], U8, name="s4", align_bytes=64)
+        s8 = keep.tile([P, PASSES, M], U8, name="s8", align_bytes=64)
+        nc.vector.memset(s4[:].bitcast(I32), 0)
+        nc.vector.memset(s8[:].bitcast(I32), 0)
+        for tile, src in ((s4, w4_scales), (s8, w8_scales)):
+            rows = src.rearrange("a r n -> r a n").bitcast(I32)
+            for q in range(4):
+                nc.gpsimd.dma_start(tile[32 * q : 32 * q + 4].bitcast(I32), rows[4 * q : 4 * q + 4])
+
+        x_rows = xT.rearrange("(a p t) n -> a t p n", p=P, t=PACK)
+        c_rows = c.rearrange("(a p t) j -> a p t j", p=P, t=PACK)
+        xs = [[keep.tile([P, T], F32, name="x%d%d" % (a, t)) for t in range(PACK)] for a in range(PASSES)]
+        cs = [keep.tile([P, PACK, S], F32, name="c%d" % a) for a in range(PASSES)]
+        w4 = keep.tile([P, PASSES, 2 * M], U8, name="w4", align_bytes=64)
+        w8 = keep.tile([P, PASSES, 4 * M], U8, name="w8", align_bytes=64)
+
+        nc.sync.dma_start(xs[0][0][:], x_rows[0, 0])
+        nc.sync.dma_start(cs[0][:, 0:2, :], c_rows[0][:, 0:2, :])
+        nc.sync.dma_start(xs[0][1][:], x_rows[0, 1])
+        nc.sync.dma_start(cs[0][:, 2:4, :], c_rows[0][:, 2:4, :])
+        nc.sync.dma_start(xs[0][2][:], x_rows[0, 2])
+        nc.sync.dma_start(xs[0][3][:], x_rows[0, 3])
+        nc.sync.dma_start(cs[1][:], c_rows[1])
+        for t in range(PACK):
+            nc.sync.dma_start(xs[1][t][:], x_rows[1, t])
+        nc.sync.dma_start(w4[:].bitcast(I32), w4_words.rearrange("a p b -> p a b").bitcast(I32))
+        nc.sync.dma_start(w8[:].bitcast(I32), w8_words.rearrange("a p n i -> p a (n i)").bitcast(I32))
+
+        def gather(diff, a, t, g, j0, j1, o0):
+            lst = offsets[:, (g * S + j0) // STRIPE : (g * S + j1) // STRIPE]
+            nc.vector.tensor_tensor(diff[:, t, o0 : o0 + j1 - j0], xs[a][t][:].indirect(lst), cs[a][:, t, j0:j1], ALU.subtract)
+
+        def quantize(name, planes, width, copy):
+            grouped = keep.tile([P, width, PACK], BF16, name="g" + name, align_bytes=64)
+            interleave(copy, grouped[:], planes)
+            codes = keep.tile([P, width], U32, name="q" + name, align_bytes=64)
+            scales = keep.tile([P, width], U8, name="s" + name, align_bytes=64)
+            nc.vector.quantize_mx(out=codes[:].bitcast(FP8X4), scales=scales[:], in_=grouped[:].rearrange("p w t -> p (w t)"))
+            return codes, scales
+
+        edge = [[psum.tile([P, M], F32, name="e%d%d" % (g, jt)) for jt in range(J_TILES)] for g in range(G)]
+        own = [psum.tile([P, M], F32, name="o%d" % jt) for jt in range(J_TILES)]
+
+        def mm(acc, codes, scales, cols, w, wdt, ws, a):
+            nc.tensor.matmul_mx(out=acc[:], lhsT=codes[:, cols].bitcast(FP8X4), lhsT_scale=scales[:, cols],
+                                rhs=w[:, a, :].bitcast(wdt), rhs_scale=ws[:, a, :], start=(a == 0), stop=(a == PASSES - 1))
+
+        d0 = [keep.tile([P, PACK, S], F32, name="d0%d" % g) for g in range(G)]
+        for t in range(PACK):
+            for g in range(G):
+                gather(d0[g], 0, t, g, 0, S, 0)
+        qc = [quantize("c%d" % a, cs[a][:], S, nc.scalar.copy) for a in range(PASSES)]
+        q0 = [quantize("d0%d" % g, d0[g][:], S, nc.scalar.copy) for g in range(G)]
+
+        d1 = [keep.tile([P, PACK, S], F32, name="d1%d" % g) for g in range(G)]
+        for t in range(2):
+            for g in range(G):
+                gather(d1[g], 1, t, g, 0, S, 0)
+        for jt in range(J_TILES):
+            cols = slice(jt * J_TILE, (jt + 1) * J_TILE)
+            for g in range(G):
+                mm(edge[g][jt], q0[g][0], q0[g][1], cols, w4, FP4X4, s4, 0)
+        for jt in range(J_TILES):
+            cols = slice(jt * J_TILE, (jt + 1) * J_TILE)
+            for a in range(PASSES):
+                mm(own[jt], qc[a][0], qc[a][1], cols, w8, FP8X4, s8, a)
+        for jt in range(J_TILES):
+            j0, j1 = jt * J_TILE, (jt + 1) * J_TILE
+            for g in range(G):
+                for t in range(2, PACK):
+                    gather(d1[g], 1, t, g, j0, j1, j0)
+                codes, scales = quantize("d1%d%d" % (g, jt), d1[g][:, :, j0:j1], J_TILE, nc.scalar.copy)
+                mm(edge[g][jt], codes, scales, slice(0, J_TILE), w4, FP4X4, s4, 1)
+            first = keep.tile([P, M], F32, name="first%d" % jt)
+            nc.scalar.copy(first[:], edge[0][jt][:])
+            best = keep.tile([P, M], F32, name="best%d" % jt)
+            nc.vector.tensor_tensor(best[:], edge[1][jt][:], first[:], ALU.max)
+            res = keep.tile([P, M], F32, name="res%d" % jt)
+            nc.vector.tensor_tensor(res[:], own[jt][:], best[:], ALU.add)
+            nc.sync.dma_start(out[j0:j1, :], res[:])

@@ -51,34 +51,38 @@ def tile_list_edge_tm_none_kernel(tc, xT, c, w4_words, w4_scales, w8_words, w8_s
 
         x_rows = xT.rearrange("(a p t) n -> a t p n", p=P, t=PACK)
         c_rows = c.rearrange("(a p t) j -> a p t j", p=P, t=PACK)
-        xs = [[keep.tile([P, T], F32, name="x%d%d" % (a, t)) for t in range(PACK)] for a in range(PASSES)]
+        xs = [[keep.tile([P, T], F32, name="x%d%d" % (a, t), tag="x%d%d" % (a, t), align_bytes=64) for t in range(PACK)] for a in range(PASSES)]
         cs = [keep.tile([P, PACK, S], F32, name="c%d" % a) for a in range(PASSES)]
         w4 = keep.tile([P, PASSES, 2 * M], U8, name="w4", align_bytes=64)
         w8 = keep.tile([P, PASSES, 4 * M], U8, name="w8", align_bytes=64)
 
-        nc.sync.dma_start(xs[0][0][:], x_rows[0, 0])
-        nc.sync.dma_start(cs[0][:, 0:2, :], c_rows[0][:, 0:2, :])
-        nc.sync.dma_start(xs[0][1][:], x_rows[0, 1])
-        nc.sync.dma_start(cs[0][:, 2:4, :], c_rows[0][:, 2:4, :])
-        nc.sync.dma_start(xs[0][2][:], x_rows[0, 2])
-        nc.sync.dma_start(xs[0][3][:], x_rows[0, 3])
-        nc.sync.dma_start(cs[1][:], c_rows[1])
-        for t in range(PACK):
-            nc.sync.dma_start(xs[1][t][:], x_rows[1, t])
-        nc.sync.dma_start(w4[:].bitcast(I32), w4_words.rearrange("a p b -> p a b").bitcast(I32))
+        for a in range(PASSES):
+            for t in range(PACK):
+                if a == PASSES - 1 and t == PACK - 1:
+                    nc.sync.dma_start(w4[:].bitcast(I32), w4_words.rearrange("a p b -> p a b").bitcast(I32))
+                nc.sync.dma_start(xs[a][t][:], x_rows[a, t])
+                if a == 0 and t < 2:
+                    nc.sync.dma_start(cs[0][:, 2 * t : 2 * t + 2, :], c_rows[0][:, 2 * t : 2 * t + 2, :])
+                if (a, t) == (0, 3):
+                    nc.sync.dma_start(cs[1][:, 0:2, :], c_rows[1][:, 0:2, :])
+                if (a, t) == (1, 0):
+                    nc.sync.dma_start(cs[1][:, 2:4, :], c_rows[1][:, 2:4, :])
         nc.sync.dma_start(w8[:].bitcast(I32), w8_words.rearrange("a p n i -> p a (n i)").bitcast(I32))
 
-        def gather(diff, a, t, g, j0, j1, o0):
+        def gather(diff, a, t, g, j0, j1):
             lst = offsets[:, (g * S + j0) // STRIPE : (g * S + j1) // STRIPE]
-            nc.vector.tensor_tensor(diff[:, t, o0 : o0 + j1 - j0], xs[a][t][:].indirect(lst), cs[a][:, t, j0:j1], ALU.subtract)
+            nc.vector.tensor_tensor(diff[:, t, j0:j1], xs[a][t][:].indirect(lst), cs[a][:, t, j0:j1], ALU.subtract)
 
-        def quantize(name, planes, width, copy):
-            grouped = keep.tile([P, width, PACK], BF16, name="g" + name, align_bytes=64)
-            interleave(copy, grouped[:], planes)
-            codes = keep.tile([P, width], U32, name="q" + name, align_bytes=64)
+        def quantize(name, grouped, width, tag):
+            codes = keep.tile([P, width], U32, name="q" + name, tag=tag, align_bytes=64)
             scales = keep.tile([P, width], U8, name="s" + name, align_bytes=64)
-            nc.vector.quantize_mx(out=codes[:].bitcast(FP8X4), scales=scales[:], in_=grouped[:].rearrange("p w t -> p (w t)"))
+            nc.vector.quantize_mx(out=codes[:].bitcast(FP8X4), scales=scales[:], in_=grouped.rearrange("p w t -> p (w t)"))
             return codes, scales
+
+        def group_all(name, planes):
+            grouped = keep.tile([P, S, PACK], BF16, name="g" + name, align_bytes=64)
+            interleave(nc.scalar.copy, grouped[:], planes)
+            return grouped
 
         edge = [[psum.tile([P, M], F32, name="e%d%d" % (g, jt)) for jt in range(J_TILES)] for g in range(G)]
         own = [psum.tile([P, M], F32, name="o%d" % jt) for jt in range(J_TILES)]
@@ -88,35 +92,58 @@ def tile_list_edge_tm_none_kernel(tc, xT, c, w4_words, w4_scales, w8_words, w8_s
                                 rhs=w[:, a, :].bitcast(wdt), rhs_scale=ws[:, a, :], start=(a == 0), stop=(a == PASSES - 1))
 
         d0 = [keep.tile([P, PACK, S], F32, name="d0%d" % g) for g in range(G)]
+        d1 = [keep.tile([P, PACK, S], F32, name="d1%d" % g) for g in range(G)]
         for t in range(PACK):
             for g in range(G):
-                gather(d0[g], 0, t, g, 0, S, 0)
-        qc = [quantize("c%d" % a, cs[a][:], S, nc.scalar.copy) for a in range(PASSES)]
-        q0 = [quantize("d0%d" % g, d0[g][:], S, nc.scalar.copy) for g in range(G)]
-
-        d1 = [keep.tile([P, PACK, S], F32, name="d1%d" % g) for g in range(G)]
+                gather(d0[g], 0, t, g, 0, S)
+        qc0 = quantize("c0", group_all("c0", cs[0][:])[:], S, "qc0")
+        g0 = [group_all("d0%d" % g, d0[g][:]) for g in range(G)]
+        gc1 = group_all("c1", cs[1][:])
+        q0 = []
         for t in range(2):
             for g in range(G):
-                gather(d1[g], 1, t, g, 0, S, 0)
+                gather(d1[g], 1, t, g, 0, S)
+            q0.append(quantize("d0%d" % t, g0[t][:], S, "x1%d" % t))
+        g1 = [keep.tile([P, S, PACK], BF16, name="gd1%d" % g, tag="gd1%d" % g, align_bytes=64) for g in range(G)]
+        for g in range(G):
+            nc.scalar.copy(g1[g][:, :, 0:2], d1[g][:, 0:2, :].rearrange("p t j -> p j t"))
+        for g in range(G):
+            gather(d1[g], 1, 2, g, 0, S)
         for jt in range(J_TILES):
             cols = slice(jt * J_TILE, (jt + 1) * J_TILE)
             for g in range(G):
                 mm(edge[g][jt], q0[g][0], q0[g][1], cols, w4, FP4X4, s4, 0)
         for jt in range(J_TILES):
             cols = slice(jt * J_TILE, (jt + 1) * J_TILE)
-            for a in range(PASSES):
-                mm(own[jt], qc[a][0], qc[a][1], cols, w8, FP8X4, s8, a)
+            mm(own[jt], qc0[0], qc0[1], cols, w8, FP8X4, s8, 0)
         for jt in range(J_TILES):
             j0, j1 = jt * J_TILE, (jt + 1) * J_TILE
             for g in range(G):
-                for t in range(2, PACK):
-                    gather(d1[g], 1, t, g, j0, j1, j0)
-                codes, scales = quantize("d1%d%d" % (g, jt), d1[g][:, :, j0:j1], J_TILE, nc.scalar.copy)
+                gather(d1[g], 1, 3, g, j0, j1)
+                nc.scalar.copy(g1[g][:, j0:j1, 2:4], d1[g][:, 2:4, j0:j1].rearrange("p t j -> p j t"))
+        for jt in range(J_TILES):
+            j0, j1 = jt * J_TILE, (jt + 1) * J_TILE
+            for g in range(G):
+                codes, scales = quantize("d1%d%d" % (g, jt), g1[g][:, j0:j1, :], J_TILE, "qd1%d%d" % (g, jt))
                 mm(edge[g][jt], codes, scales, slice(0, J_TILE), w4, FP4X4, s4, 1)
+                if (jt, g) == (J_TILES - 1, 0):
+                    qc1 = quantize("c1", gc1[:], S, "gd10")
+        for jt in range(J_TILES):
+            mm(own[jt], qc1[0], qc1[1], slice(jt * J_TILE, (jt + 1) * J_TILE), w8, FP8X4, s8, 1)
+        H = M // 2
+        for jt in range(J_TILES):
+            j0, j1 = jt * J_TILE, (jt + 1) * J_TILE
             first = keep.tile([P, M], F32, name="first%d" % jt)
             nc.scalar.copy(first[:], edge[0][jt][:])
             best = keep.tile([P, M], F32, name="best%d" % jt)
-            nc.vector.tensor_tensor(best[:], edge[1][jt][:], first[:], ALU.max)
             res = keep.tile([P, M], F32, name="res%d" % jt)
-            nc.vector.tensor_tensor(res[:], own[jt][:], best[:], ALU.add)
-            nc.sync.dma_start(out[j0:j1, :], res[:])
+            for h in range(2):
+                n = slice(h * H, (h + 1) * H)
+                nc.vector.tensor_tensor(best[:, n], edge[1][jt][:, n], first[:, n], ALU.max)
+            for h in range(2):
+                n = slice(h * H, (h + 1) * H)
+                nc.vector.tensor_tensor(res[:, n], own[jt][:, n], best[:, n], ALU.add)
+                if jt == J_TILES - 1:
+                    nc.sync.dma_start(out[j0:j1, n], res[:, n])
+            if jt < J_TILES - 1:
+                nc.sync.dma_start(out[j0:j1, :], res[:])

@@ -35,43 +35,55 @@ def tile_list_edge_tm_none_kernel(tc, xT, c, w4_words, w4_scales, w8_words, w8_s
     nc = tc.nc
     with ExitStack() as ctx:
         keep = ctx.enter_context(tc.tile_pool(name="keep", bufs=1))
+        ring = ctx.enter_context(tc.tile_pool(name="ring", bufs=2))
         psum = ctx.enter_context(tc.psum_pool(name="psum", bufs=1))
 
         offsets = keep.tile([P, G * S // STRIPE], U16, name="offsets")
-        nc.sync.dma_start(offsets[:], offs)
 
         s4 = keep.tile([P, PASSES, M], U8, name="s4", align_bytes=64)
         s8 = keep.tile([P, PASSES, M], U8, name="s8", align_bytes=64)
         nc.vector.memset(s4[:].bitcast(I32), 0)
         nc.vector.memset(s8[:].bitcast(I32), 0)
-        for tile, src in ((s4, w4_scales), (s8, w8_scales)):
+
+        def load_scales(queue, tile, src):
             rows = src.rearrange("a r n -> r a n").bitcast(I32)
             for q in range(4):
-                nc.gpsimd.dma_start(tile[32 * q : 32 * q + 4].bitcast(I32), rows[4 * q : 4 * q + 4])
+                queue.dma_start(tile[32 * q : 32 * q + 4].bitcast(I32), rows[4 * q : 4 * q + 4])
+
+        load_scales(nc.gpsimd, s4, w4_scales)
 
         x_rows = xT.rearrange("(a p t) n -> a t p n", p=P, t=PACK)
         c_rows = c.rearrange("(a p t) j -> a p t j", p=P, t=PACK)
         xs = [[keep.tile([P, T], F32, name="x%d%d" % (a, t), tag="x%d%d" % (a, t), align_bytes=64) for t in range(PACK)] for a in range(PASSES)]
         cs = [keep.tile([P, PACK, S], F32, name="c%d" % a) for a in range(PASSES)]
-        w4 = keep.tile([P, PASSES, 2 * M], U8, name="w4", align_bytes=64)
+        w4 = [keep.tile([P, 2 * M], U8, name="w4%d" % a, align_bytes=64) for a in range(PASSES)]
         w8 = keep.tile([P, PASSES, 4 * M], U8, name="w8", align_bytes=64)
 
-        for a in range(PASSES):
-            for t in range(PACK):
-                if a == PASSES - 1 and t == PACK - 1:
-                    nc.sync.dma_start(w4[:].bitcast(I32), w4_words.rearrange("a p b -> p a b").bitcast(I32))
-                nc.sync.dma_start(xs[a][t][:], x_rows[a, t])
-                if a == 0 and t < 2:
-                    nc.sync.dma_start(cs[0][:, 2 * t : 2 * t + 2, :], c_rows[0][:, 2 * t : 2 * t + 2, :])
-                if (a, t) == (0, 3):
-                    nc.sync.dma_start(cs[1][:, 0:2, :], c_rows[1][:, 0:2, :])
-                if (a, t) == (1, 0):
-                    nc.sync.dma_start(cs[1][:, 2:4, :], c_rows[1][:, 2:4, :])
+        w4_rows = w4_words.rearrange("a p b -> p a b").bitcast(I32)
+        nc.sync.dma_start(xs[0][0][:], x_rows[0, 0])
+        nc.sync.dma_start(offsets[:], offs)
+        nc.sync.dma_start(cs[0][:, 0:1, :], c_rows[0][:, 0:1, :])
+        nc.sync.dma_start(xs[0][1][:], x_rows[0, 1])
+        nc.sync.dma_start(cs[0][:, 1:2, :], c_rows[0][:, 1:2, :])
+        nc.sync.dma_start(xs[0][2][:], x_rows[0, 2])
+        nc.sync.dma_start(cs[0][:, 2:4, :], c_rows[0][:, 2:4, :])
+        nc.sync.dma_start(xs[0][3][:], x_rows[0, 3])
+        nc.sync.dma_start(cs[1][:, 0:2, :], c_rows[1][:, 0:2, :])
+        nc.sync.dma_start(xs[1][0][:], x_rows[1, 0])
+        nc.sync.dma_start(cs[1][:, 2:4, :], c_rows[1][:, 2:4, :])
+        nc.sync.dma_start(xs[1][1][:], x_rows[1, 1])
+        nc.sync.dma_start(xs[1][2][:], x_rows[1, 2])
+        nc.sync.dma_start(w4[0][:].bitcast(I32), w4_rows[:, 0, :])
+        nc.sync.dma_start(xs[1][3][:], x_rows[1, 3])
+        load_scales(nc.sync, s8, w8_scales)
         nc.sync.dma_start(w8[:].bitcast(I32), w8_words.rearrange("a p n i -> p a (n i)").bitcast(I32))
+        nc.sync.dma_start(w4[1][:].bitcast(I32), w4_rows[:, 1, :])
+        w4_ops = [w4[a][:] for a in range(PASSES)]
+        w8_ops = [w8[:, a, :] for a in range(PASSES)]
 
-        def gather(diff, a, t, g, j0, j1):
+        def gather(dst, a, t, g, j0, j1):
             lst = offsets[:, (g * S + j0) // STRIPE : (g * S + j1) // STRIPE]
-            nc.vector.tensor_tensor(diff[:, t, j0:j1], xs[a][t][:].indirect(lst), cs[a][:, t, j0:j1], ALU.subtract)
+            nc.vector.tensor_tensor(dst, xs[a][t][:].indirect(lst), cs[a][:, t, j0:j1], ALU.subtract)
 
         def quantize(name, grouped, width, tag):
             codes = keep.tile([P, width], U32, name="q" + name, tag=tag, align_bytes=64)
@@ -89,56 +101,55 @@ def tile_list_edge_tm_none_kernel(tc, xT, c, w4_words, w4_scales, w8_words, w8_s
 
         def mm(acc, codes, scales, cols, w, wdt, ws, a):
             nc.tensor.matmul_mx(out=acc[:], lhsT=codes[:, cols].bitcast(FP8X4), lhsT_scale=scales[:, cols],
-                                rhs=w[:, a, :].bitcast(wdt), rhs_scale=ws[:, a, :], start=(a == 0), stop=(a == PASSES - 1))
+                                rhs=w[a].bitcast(wdt), rhs_scale=ws[:, a, :], start=(a == 0), stop=(a == PASSES - 1))
 
-        d0 = [keep.tile([P, PACK, S], F32, name="d0%d" % g) for g in range(G)]
-        d1 = [keep.tile([P, PACK, S], F32, name="d1%d" % g) for g in range(G)]
-        for t in range(PACK):
+        d0 = [keep.tile([P, PACK, S], F32, name="d0%d" % g, tag="d0%d" % g, align_bytes=64) for g in range(G)]
+        d1 = [keep.tile([P, 2, S], F32, name="d1%d" % g) for g in range(G)]
+        g0 = [keep.tile([P, S, PACK], BF16, name="gd0%d" % g, align_bytes=64) for g in range(G)]
+        g1 = [keep.tile([P, S, PACK], BF16, name="gd1%d" % g, align_bytes=64) for g in range(G)]
+        for u in range(2):
+            for t in range(2 * u, 2 * u + 2):
+                for g in range(G):
+                    gather(d0[g][:, t, :], 0, t, g, 0, S)
             for g in range(G):
-                gather(d0[g], 0, t, g, 0, S)
-        qc0 = quantize("c0", group_all("c0", cs[0][:])[:], S, "qc0")
-        g0 = [group_all("d0%d" % g, d0[g][:]) for g in range(G)]
-        gc1 = group_all("c1", cs[1][:])
-        q0 = []
+                nc.scalar.copy(g0[g][:, :, 2 * u : 2 * u + 2], d0[g][:, 2 * u : 2 * u + 2, :].rearrange("p t j -> p j t"))
+            if u == 0:
+                gc0 = group_all("c0", cs[0][:])
+        qc0 = quantize("c0", gc0[:], S, "d00")
+        q0 = [quantize("d0%d" % g, g0[g][:], S, "qd0%d" % g) for g in range(G)]
+        qc1 = quantize("c1", group_all("c1", cs[1][:])[:], S, "qc1")
         for t in range(2):
             for g in range(G):
-                gather(d1[g], 1, t, g, 0, S)
-            q0.append(quantize("d0%d" % t, g0[t][:], S, "x1%d" % t))
-        g1 = [keep.tile([P, S, PACK], BF16, name="gd1%d" % g, tag="gd1%d" % g, align_bytes=64) for g in range(G)]
+                gather(d1[g][:, t, :], 1, t, g, 0, S)
         for g in range(G):
-            nc.scalar.copy(g1[g][:, :, 0:2], d1[g][:, 0:2, :].rearrange("p t j -> p j t"))
-        for g in range(G):
-            gather(d1[g], 1, 2, g, 0, S)
+            nc.scalar.copy(g1[g][:, :, 0:2], d1[g][:].rearrange("p t j -> p j t"))
         for jt in range(J_TILES):
             cols = slice(jt * J_TILE, (jt + 1) * J_TILE)
             for g in range(G):
-                mm(edge[g][jt], q0[g][0], q0[g][1], cols, w4, FP4X4, s4, 0)
+                mm(edge[g][jt], q0[g][0], q0[g][1], cols, w4_ops, FP4X4, s4, 0)
         for jt in range(J_TILES):
             cols = slice(jt * J_TILE, (jt + 1) * J_TILE)
-            mm(own[jt], qc0[0], qc0[1], cols, w8, FP8X4, s8, 0)
-        for jt in range(J_TILES):
-            j0, j1 = jt * J_TILE, (jt + 1) * J_TILE
-            for g in range(G):
-                gather(d1[g], 1, 3, g, j0, j1)
-                nc.scalar.copy(g1[g][:, j0:j1, 2:4], d1[g][:, 2:4, j0:j1].rearrange("p t j -> p j t"))
-        for jt in range(J_TILES):
-            j0, j1 = jt * J_TILE, (jt + 1) * J_TILE
-            for g in range(G):
-                codes, scales = quantize("d1%d%d" % (g, jt), g1[g][:, j0:j1, :], J_TILE, "qd1%d%d" % (g, jt))
-                mm(edge[g][jt], codes, scales, slice(0, J_TILE), w4, FP4X4, s4, 1)
-                if (jt, g) == (J_TILES - 1, 0):
-                    qc1 = quantize("c1", gc1[:], S, "gd10")
-        for jt in range(J_TILES):
-            mm(own[jt], qc1[0], qc1[1], slice(jt * J_TILE, (jt + 1) * J_TILE), w8, FP8X4, s8, 1)
+            mm(own[jt], qc0[0], qc0[1], cols, w8_ops, FP8X4, s8, 0)
+            mm(own[jt], qc1[0], qc1[1], cols, w8_ops, FP8X4, s8, 1)
         H = M // 2
         for jt in range(J_TILES):
             j0, j1 = jt * J_TILE, (jt + 1) * J_TILE
+            for g in range(G):
+                pair = ring.tile([P, 2, J_TILE], F32, name="pair")
+                for t in range(2):
+                    gather(pair[:, t, :], 1, 2 + t, g, j0, j1)
+                copy = nc.vector.tensor_copy if (jt, g) == (J_TILES - 1, G - 1) else nc.scalar.copy
+                copy(g1[g][:, j0:j1, 2:4], pair[:].rearrange("p t j -> p j t"))
+                codes, scales = quantize("d1%d%d" % (g, jt), g1[g][:, j0:j1, :], J_TILE, "qd1%d%d" % (g, jt))
+                mm(edge[g][jt], codes, scales, slice(0, J_TILE), w4_ops, FP4X4, s4, 1)
+        for jt in range(J_TILES):
+            j0, j1 = jt * J_TILE, (jt + 1) * J_TILE
             first = keep.tile([P, M], F32, name="first%d" % jt)
-            nc.scalar.copy(first[:], edge[0][jt][:])
             best = keep.tile([P, M], F32, name="best%d" % jt)
             res = keep.tile([P, M], F32, name="res%d" % jt)
             for h in range(2):
                 n = slice(h * H, (h + 1) * H)
+                nc.scalar.copy(first[:, n], edge[0][jt][:, n])
                 nc.vector.tensor_tensor(best[:, n], edge[1][jt][:, n], first[:, n], ALU.max)
             for h in range(2):
                 n = slice(h * H, (h + 1) * H)

@@ -1,6 +1,7 @@
 from contextlib import ExitStack
 
 import concourse.mybir as mybir
+from concourse.masks import make_identity
 
 G, K, M, T, S = 2, 1024, 512, 1024, 256
 FLOPS = 2 * K * M * S * (G + 1)
@@ -50,6 +51,8 @@ def tile_list_edge_tm_none_kernel(tc, xT, c, w4_words, w4_scales, w8_words, w8_s
             for q in range(4):
                 queue.dma_start(tile[32 * q : 32 * q + 4].bitcast(I32), rows[4 * q : 4 * q + 4])
 
+        ident = keep.tile([P, P], F32, name="ident")
+        make_identity(nc, ident[:])
         load_scales(nc.gpsimd, s4, w4_scales)
 
         x_rows = xT.rearrange("(a p t) n -> a t p n", p=P, t=PACK)
@@ -97,7 +100,6 @@ def tile_list_edge_tm_none_kernel(tc, xT, c, w4_words, w4_scales, w8_words, w8_s
             return grouped
 
         edge = [[psum.tile([P, M], F32, name="e%d%d" % (g, jt)) for jt in range(J_TILES)] for g in range(G)]
-        own = [psum.tile([P, M], F32, name="o%d" % jt) for jt in range(J_TILES)]
 
         def mm(acc, codes, scales, cols, w, wdt, ws, a):
             nc.tensor.matmul_mx(out=acc[:], lhsT=codes[:, cols].bitcast(FP8X4), lhsT_scale=scales[:, cols],
@@ -107,25 +109,47 @@ def tile_list_edge_tm_none_kernel(tc, xT, c, w4_words, w4_scales, w8_words, w8_s
         d1 = [keep.tile([P, 2, S], F32, name="d1%d" % g) for g in range(G)]
         g0 = [keep.tile([P, S, PACK], BF16, name="gd0%d" % g, align_bytes=64) for g in range(G)]
         g1 = [keep.tile([P, S, PACK], BF16, name="gd1%d" % g, align_bytes=64) for g in range(G)]
+        neg = keep.tile([P, PACK, S], F32, name="neg")
+        for t0, t1 in ((0, 1), (1, 2), (2, 4)):
+            nc.scalar.activation(neg[:, t0:t1, :], cs[0][:, t0:t1, :], mybir.ActivationFunctionType.Copy, scale=-1.0)
+        turned = [psum.tile([P, PACK, P], F32, name="turned%d" % jt) for jt in range(J_TILES)]
         for u in range(2):
             for t in range(2 * u, 2 * u + 2):
-                for g in range(G):
-                    gather(d0[g][:, t, :], 0, t, g, 0, S)
-            for g in range(G):
-                nc.scalar.copy(g0[g][:, :, 2 * u : 2 * u + 2], d0[g][:, 2 * u : 2 * u + 2, :].rearrange("p t j -> p j t"))
+                gather(d0[1][:, t, :], 0, t, 1, 0, S)
+                nc.vector.tensor_copy(d0[0][:, t, :], xs[0][t][:].indirect(offsets[:, 0 : S // STRIPE]))
+                for jt in range(J_TILES):
+                    cols = slice(jt * J_TILE, (jt + 1) * J_TILE)
+                    nc.tensor.matmul(turned[jt][:, t, :], lhsT=neg[:, t, cols], rhs=ident[:], start=True, stop=False, is_transpose=True)
+                    nc.tensor.matmul(turned[jt][:, t, :], lhsT=d0[0][:, t, cols], rhs=ident[:], start=False, stop=True, is_transpose=True)
             if u == 0:
+                nc.scalar.copy(g0[1][:, :, 0:2], d0[1][:, 0:2, :].rearrange("p t j -> p j t"))
                 gc0 = group_all("c0", cs[0][:])
-        qc0 = quantize("c0", gc0[:], S, "d00")
-        q0 = [quantize("d0%d" % g, g0[g][:], S, "qd0%d" % g) for g in range(G)]
-        qc1 = quantize("c1", group_all("c1", cs[1][:])[:], S, "qc1")
+        nc.scalar.copy(g0[1][:, :, 2:4], d0[1][:, 2:4, :].rearrange("p t j -> p j t"))
+        back = psum.tile([P, J_TILES, 2, J_TILE], F32, name="back", tag="o1")
+        for jt in range(J_TILES):
+            rows = keep.tile([P, 2, P, 2], BF16, name="rows%d" % jt)
+            nc.scalar.copy(rows[:], turned[jt][:].rearrange("j (u e) p -> j u p e", e=2))
+            words = rows[:].rearrange("j u p e -> j (u p e)").bitcast(F32)
+            for u in range(2):
+                nc.tensor.transpose(back[:, jt, u, :], words[:, u * P : (u + 1) * P], ident[:])
+        nc.scalar.copy(
+            g0[0][:].rearrange("p j t -> p (j t)").bitcast(F32).rearrange("p (jt j u) -> p jt j u", jt=J_TILES, u=2),
+            back[:].rearrange("p jt u j -> p jt j u"),
+        )
+        own = [psum.tile([P, M], F32, name="o%d" % jt, tag="o%d" % jt) for jt in range(J_TILES)]
+        qc0 = quantize("c0", gc0[:], S, "qc0")
+        q01 = quantize("d01", g0[1][:], S, "qd01")
+        gc1 = group_all("c1", cs[1][:])
         for t in range(2):
             for g in range(G):
                 gather(d1[g][:, t, :], 1, t, g, 0, S)
+        qc1 = quantize("c1", gc1[:], S, "qc1")
+        q0 = [quantize("d00", g0[0][:], S, "x11"), q01]
         for g in range(G):
             nc.scalar.copy(g1[g][:, :, 0:2], d1[g][:].rearrange("p t j -> p j t"))
-        for jt in range(J_TILES):
-            cols = slice(jt * J_TILE, (jt + 1) * J_TILE)
-            for g in range(G):
+        for g in (1, 0):
+            for jt in range(J_TILES):
+                cols = slice(jt * J_TILE, (jt + 1) * J_TILE)
                 mm(edge[g][jt], q0[g][0], q0[g][1], cols, w4_ops, FP4X4, s4, 0)
         for jt in range(J_TILES):
             cols = slice(jt * J_TILE, (jt + 1) * J_TILE)

from contextlib import ExitStack

import concourse.mybir as mybir
from concourse.masks import make_identity

G, K, M, T, S = 2, 1024, 512, 1024, 256
FLOPS = 2 * K * M * S * (G + 1)

F32 = mybir.dt.float32
BF16 = mybir.dt.bfloat16
I32 = mybir.dt.int32
U32 = mybir.dt.uint32
U16 = mybir.dt.uint16
U8 = mybir.dt.uint8
FP8X4 = mybir.dt.float8_e4m3fn_x4
FP4X4 = mybir.dt.float4_e2m1fn_x4
ALU = mybir.AluOpType

P = 128
PACK = 4
K_PASS = P * PACK
PASSES = K // K_PASS
J_TILE = 128
J_TILES = S // J_TILE
STRIPE = 16


def interleave(engine_copy, grouped, planes):
    engine_copy(
        grouped.rearrange("p (c i) t -> p c t i", i=4),
        planes.rearrange("p t (c i) -> p c t i", i=4),
    )


def tile_list_edge_tm_none_kernel(tc, xT, c, w4_words, w4_scales, w8_words, w8_scales, offs, out):
    nc = tc.nc
    with ExitStack() as ctx:
        keep = ctx.enter_context(tc.tile_pool(name="keep", bufs=1))
        ring = ctx.enter_context(tc.tile_pool(name="ring", bufs=2))
        psum = ctx.enter_context(tc.psum_pool(name="psum", bufs=1))

        offsets = keep.tile([P, G * S // STRIPE], U16, name="offsets")

        s4 = keep.tile([P, PASSES, M], U8, name="s4", align_bytes=64)
        s8 = keep.tile([P, PASSES, M], U8, name="s8", align_bytes=64)
        nc.vector.memset(s4[:].bitcast(I32), 0)
        nc.vector.memset(s8[:].bitcast(I32), 0)

        def load_scales(queue, tile, src):
            rows = src.rearrange("a r n -> r a n").bitcast(I32)
            for q in range(4):
                queue.dma_start(tile[32 * q : 32 * q + 4].bitcast(I32), rows[4 * q : 4 * q + 4])

        ident = keep.tile([P, P], F32, name="ident")
        make_identity(nc, ident[:])
        load_scales(nc.gpsimd, s4, w4_scales)

        x_rows = xT.rearrange("(a p t) n -> a t p n", p=P, t=PACK)
        c_rows = c.rearrange("(a p t) j -> a p t j", p=P, t=PACK)
        xs = [[keep.tile([P, T], F32, name="x%d%d" % (a, t), tag="x%d%d" % (a, t), align_bytes=64) for t in range(PACK)] for a in range(PASSES)]
        cs = [keep.tile([P, PACK, S], F32, name="c%d" % a) for a in range(PASSES)]
        w4 = [keep.tile([P, 2 * M], U8, name="w4%d" % a, align_bytes=64) for a in range(PASSES)]
        w8 = keep.tile([P, PASSES, 4 * M], U8, name="w8", align_bytes=64)

        w4_rows = w4_words.rearrange("a p b -> p a b").bitcast(I32)
        nc.sync.dma_start(xs[0][0][:], x_rows[0, 0])
        nc.sync.dma_start(offsets[:], offs)
        nc.sync.dma_start(cs[0][:, 0:1, :], c_rows[0][:, 0:1, :])
        nc.sync.dma_start(xs[0][1][:], x_rows[0, 1])
        nc.sync.dma_start(cs[0][:, 1:2, :], c_rows[0][:, 1:2, :])
        nc.sync.dma_start(xs[0][2][:], x_rows[0, 2])
        nc.sync.dma_start(cs[0][:, 2:4, :], c_rows[0][:, 2:4, :])
        nc.sync.dma_start(xs[0][3][:], x_rows[0, 3])
        nc.sync.dma_start(cs[1][:, 0:2, :], c_rows[1][:, 0:2, :])
        nc.sync.dma_start(xs[1][0][:], x_rows[1, 0])
        nc.sync.dma_start(cs[1][:, 2:4, :], c_rows[1][:, 2:4, :])
        nc.sync.dma_start(xs[1][1][:], x_rows[1, 1])
        nc.sync.dma_start(xs[1][2][:], x_rows[1, 2])
        nc.sync.dma_start(w4[0][:].bitcast(I32), w4_rows[:, 0, :])
        nc.sync.dma_start(xs[1][3][:], x_rows[1, 3])
        load_scales(nc.sync, s8, w8_scales)
        nc.sync.dma_start(w8[:].bitcast(I32), w8_words.rearrange("a p n i -> p a (n i)").bitcast(I32))
        nc.sync.dma_start(w4[1][:].bitcast(I32), w4_rows[:, 1, :])
        w4_ops = [w4[a][:] for a in range(PASSES)]
        w8_ops = [w8[:, a, :] for a in range(PASSES)]

        def gather(dst, a, t, g, j0, j1):
            lst = offsets[:, (g * S + j0) // STRIPE : (g * S + j1) // STRIPE]
            nc.vector.tensor_tensor(dst, xs[a][t][:].indirect(lst), cs[a][:, t, j0:j1], ALU.subtract)

        def quantize(name, grouped, width, tag):
            codes = keep.tile([P, width], U32, name="q" + name, tag=tag, align_bytes=64)
            scales = keep.tile([P, width], U8, name="s" + name, align_bytes=64)
            nc.vector.quantize_mx(out=codes[:].bitcast(FP8X4), scales=scales[:], in_=grouped.rearrange("p w t -> p (w t)"))
            return codes, scales

        def group_all(name, planes):
            grouped = keep.tile([P, S, PACK], BF16, name="g" + name, align_bytes=64)
            interleave(nc.scalar.copy, grouped[:], planes)
            return grouped

        edge = [[psum.tile([P, M], F32, name="e%d%d" % (g, jt)) for jt in range(J_TILES)] for g in range(G)]

        def mm(acc, codes, scales, cols, w, wdt, ws, a):
            nc.tensor.matmul_mx(out=acc[:], lhsT=codes[:, cols].bitcast(FP8X4), lhsT_scale=scales[:, cols],
                                rhs=w[a].bitcast(wdt), rhs_scale=ws[:, a, :], start=(a == 0), stop=(a == PASSES - 1))

        d0 = [keep.tile([P, PACK, S], F32, name="d0%d" % g, tag="d0%d" % g, align_bytes=64) for g in range(G)]
        d1 = [keep.tile([P, 2, S], F32, name="d1%d" % g) for g in range(G)]
        g0 = [keep.tile([P, S, PACK], BF16, name="gd0%d" % g, align_bytes=64) for g in range(G)]
        g1 = [keep.tile([P, S, PACK], BF16, name="gd1%d" % g, align_bytes=64) for g in range(G)]
        neg = keep.tile([P, PACK, S], F32, name="neg")
        for t0, t1 in ((0, 1), (1, 2), (2, 4)):
            nc.scalar.activation(neg[:, t0:t1, :], cs[0][:, t0:t1, :], mybir.ActivationFunctionType.Copy, scale=-1.0)
        turned = [psum.tile([P, PACK, P], F32, name="turned%d" % jt) for jt in range(J_TILES)]
        for u in range(2):
            for t in range(2 * u, 2 * u + 2):
                gather(d0[1][:, t, :], 0, t, 1, 0, S)
                nc.vector.tensor_copy(d0[0][:, t, :], xs[0][t][:].indirect(offsets[:, 0 : S // STRIPE]))
                for jt in range(J_TILES):
                    cols = slice(jt * J_TILE, (jt + 1) * J_TILE)
                    nc.tensor.matmul(turned[jt][:, t, :], lhsT=neg[:, t, cols], rhs=ident[:], start=True, stop=False, is_transpose=True)
                    nc.tensor.matmul(turned[jt][:, t, :], lhsT=d0[0][:, t, cols], rhs=ident[:], start=False, stop=True, is_transpose=True)
            if u == 0:
                nc.scalar.copy(g0[1][:, :, 0:2], d0[1][:, 0:2, :].rearrange("p t j -> p j t"))
                gc0 = group_all("c0", cs[0][:])
        nc.scalar.copy(g0[1][:, :, 2:4], d0[1][:, 2:4, :].rearrange("p t j -> p j t"))
        back = psum.tile([P, J_TILES, 2, J_TILE], F32, name="back", tag="o1")
        for jt in range(J_TILES):
            rows = keep.tile([P, 2, P, 2], BF16, name="rows%d" % jt)
            nc.scalar.copy(rows[:], turned[jt][:].rearrange("j (u e) p -> j u p e", e=2))
            words = rows[:].rearrange("j u p e -> j (u p e)").bitcast(F32)
            for u in range(2):
                nc.tensor.transpose(back[:, jt, u, :], words[:, u * P : (u + 1) * P], ident[:])
        nc.scalar.copy(
            g0[0][:].rearrange("p j t -> p (j t)").bitcast(F32).rearrange("p (jt j u) -> p jt j u", jt=J_TILES, u=2),
            back[:].rearrange("p jt u j -> p jt j u"),
        )
        own = [psum.tile([P, M], F32, name="o%d" % jt, tag="o%d" % jt) for jt in range(J_TILES)]
        qc0 = quantize("c0", gc0[:], S, "qc0")
        q01 = quantize("d01", g0[1][:], S, "qd01")
        gc1 = group_all("c1", cs[1][:])
        for t in range(2):
            for g in range(G):
                gather(d1[g][:, t, :], 1, t, g, 0, S)
        qc1 = quantize("c1", gc1[:], S, "qc1")
        q0 = [quantize("d00", g0[0][:], S, "x11"), q01]
        for g in range(G):
            nc.scalar.copy(g1[g][:, :, 0:2], d1[g][:].rearrange("p t j -> p j t"))
        for g in (1, 0):
            for jt in range(J_TILES):
                cols = slice(jt * J_TILE, (jt + 1) * J_TILE)
                mm(edge[g][jt], q0[g][0], q0[g][1], cols, w4_ops, FP4X4, s4, 0)
        for jt in range(J_TILES):
            cols = slice(jt * J_TILE, (jt + 1) * J_TILE)
            mm(own[jt], qc0[0], qc0[1], cols, w8_ops, FP8X4, s8, 0)
            mm(own[jt], qc1[0], qc1[1], cols, w8_ops, FP8X4, s8, 1)
        H = M // 2
        for jt in range(J_TILES):
            j0, j1 = jt * J_TILE, (jt + 1) * J_TILE
            for g in range(G):
                pair = ring.tile([P, 2, J_TILE], F32, name="pair")
                for t in range(2):
                    gather(pair[:, t, :], 1, 2 + t, g, j0, j1)
                copy = nc.vector.tensor_copy if (jt, g) == (J_TILES - 1, G - 1) else nc.scalar.copy
                copy(g1[g][:, j0:j1, 2:4], pair[:].rearrange("p t j -> p j t"))
                codes, scales = quantize("d1%d%d" % (g, jt), g1[g][:, j0:j1, :], J_TILE, "qd1%d%d" % (g, jt))
                mm(edge[g][jt], codes, scales, slice(0, J_TILE), w4_ops, FP4X4, s4, 1)
        for jt in range(J_TILES):
            j0, j1 = jt * J_TILE, (jt + 1) * J_TILE
            first = keep.tile([P, M], F32, name="first%d" % jt)
            best = keep.tile([P, M], F32, name="best%d" % jt)
            res = keep.tile([P, M], F32, name="res%d" % jt)
            for h in range(2):
                n = slice(h * H, (h + 1) * H)
                nc.scalar.copy(first[:, n], edge[0][jt][:, n])
                nc.vector.tensor_tensor(best[:, n], edge[1][jt][:, n], first[:, n], ALU.max)
            for h in range(2):
                n = slice(h * H, (h + 1) * H)
                nc.vector.tensor_tensor(res[:, n], own[jt][:, n], best[:, n], ALU.add)
                if jt == J_TILES - 1:
                    nc.sync.dma_start(out[j0:j1, n], res[:, n])
            if jt < J_TILES - 1:
                nc.sync.dma_start(out[j0:j1, :], res[:])
